import numpy as np
import ml_dtypes


def mxq(x, axis, fmt="e4m3"):
    dtype, down = {"e4m3": (ml_dtypes.float8_e4m3fn, 7), "e5m2": (ml_dtypes.float8_e5m2, 14)}[fmt]
    v = np.moveaxis(np.asarray(x, np.float32).astype(ml_dtypes.bfloat16).astype(np.float64), axis, -1)
    blocks = v.reshape(v.shape[:-1] + (-1, 32))
    amax = np.abs(blocks).max(-1, keepdims=True)
    byte = np.maximum(np.where(amax > 0, np.frexp(amax)[1] - 1 + 127, 0) - down, 1)
    scale = np.exp2(byte - 127.0)
    codes = (blocks / scale).astype(np.float32).astype(dtype).astype(np.float64)
    return np.moveaxis((codes * scale).reshape(v.shape), -1, axis)


WIDE = False


def mx_kscale(k):
    if not WIDE:
        return np.ones(k)
    levels = np.array([10, -10, 5, -5, 0])
    if k % 512:
        return np.exp2(np.random.permutation(np.resize(levels, k // 32))).repeat(32)
    a = np.empty((k // 512, 16))
    for p in range(k // 512):
        a[p, :8] = np.random.permutation(np.resize(levels, 8))
        for g in range(8):
            far = levels[np.abs(levels - a[p, g]) >= 10]
            a[p, g + 8] = far[np.random.randint(len(far))]
    return np.exp2(a.ravel()).repeat(32)


def f64(x):
    return np.asarray(x).astype(np.float64)


E2M1 = np.array([0.0, 0.5, 1.0, 1.5, 2.0, 3.0, 4.0, 6.0, -0.0, -0.5, -1.0, -1.5, -2.0, -3.0, -4.0, -6.0])


def pack_weight(w, fmt):
    k, n = w.shape
    w = f64(np.asarray(w, np.float32).astype(ml_dtypes.bfloat16)).reshape(k // 32, 32, n)
    amax = np.abs(w).max(1)
    if fmt == "e4m3":
        byte = np.frexp(amax)[1] - 1 + 127 - 7
    else:
        mant, ex = np.frexp(amax / 6.0)
        byte = np.where(mant > 0.5, ex, ex - 1) + 127
    byte = np.clip(np.where(amax > 0, byte, 1), 1, 254)
    scaled = (w * np.exp2(127.0 - byte)[:, None, :]).reshape(k, n).astype(np.float32)
    by_word = np.ascontiguousarray(scaled.reshape(k // 512, 128, 4, n).transpose(0, 1, 3, 2))
    if fmt == "e4m3":
        words = by_word.astype(ml_dtypes.float8_e4m3fn).view(np.uint8)
    else:
        c = by_word.astype(ml_dtypes.float4_e2m1fn).view(np.uint8) & 0xF
        words = (c[..., 0::2] | (c[..., 1::2] << 4)).reshape(k // 512, 128, 2 * n)
    return np.ascontiguousarray(words), np.ascontiguousarray(byte.astype(np.uint8).reshape(k // 512, 16, n))


def unpack_weight(words, scales, fmt):
    g, _, n = scales.shape
    words = np.ascontiguousarray(words).reshape(g, 128, n, -1)
    if fmt == "e4m3":
        vals = words.view(ml_dtypes.float8_e4m3fn).astype(np.float64)
    else:
        nib = np.empty((g, 128, n, 4), np.uint8)
        nib[..., 0::2] = words & 0xF
        nib[..., 1::2] = words >> 4
        vals = E2M1[nib]
    vals = vals * np.repeat(np.exp2(scales.astype(np.float64) - 127.0), 8, axis=1)[..., None]
    return vals.transpose(0, 1, 3, 2).reshape(g * 512, n)


O, K, M, T = 1024, 3072, 1536, 512


def setup_inputs():
    n = np.random.standard_normal
    s = mx_kscale(K)[:, None]
    x = n((K, T)); x[:O] *= 6.0
    w = n((K, M)) / np.sqrt(K) / s; w[:O] /= 2.0
    p_x4 = pack_weight(x[O:] * s[O:], "e2m1")
    p_w4 = pack_weight(w[O:], "e2m1")
    return {
        "x8": (x[:O] * s[:O]).astype(np.float32),
        "w8": (w[:O]).astype(np.float32),
        "x4_words": p_x4[0],
        "x4_scales": p_x4[1],
        "w4_words": p_w4[0],
        "w4_scales": p_w4[1],
        "r": (n((1536, 512))).astype(np.float32),
    }


def reference(x8, w8, x4_words, x4_scales, w4_words, w4_scales, r):
    x8_ = mxq(f64(x8), 0, "e4m3")
    w8_ = mxq(f64(w8), 0, "e4m3")
    x4_ = unpack_weight(x4_words, x4_scales, "e2m1")
    w4_ = unpack_weight(w4_words, w4_scales, "e2m1")
    y = w8_.T @ x8_ + w4_.T @ x4_
    return f64(r) + y

@@ -1,0 +1,170 @@
+from contextlib import ExitStack
+
+import concourse.mybir as mybir
+
+F32 = mybir.dt.float32
+BF16 = mybir.dt.bfloat16
+U32 = mybir.dt.uint32
+U8 = mybir.dt.uint8
+I32 = mybir.dt.int32
+FP8X4 = mybir.dt.float8_e4m3fn_x4
+FP4X4 = mybir.dt.float4_e2m1fn_x4
+
+P = 128
+T = 512
+N = 1536
+K8 = 1024
+K4 = 2048
+PASSES8 = K8 // 512
+PASSES4 = K4 // 512
+TILES = N // P
+BANKS = 8
+GROUP = 4
+HEAD = BANKS * P
+STORE_AFTER = {3: (0, 0, 4), 7: (1, 0, 4), 9: (2, 0, 2), 10: (2, 2, 3), 11: (2, 3, 4)}
+
+FLOPS = 2 * N * T * (K8 + K4)
+
+
+def tile_mix_atom_fm_res_kernel(tc, x8, w8, x4_words, x4_scales, w4_words, w4_scales, r, out):
+    nc = tc.nc
+    with ExitStack() as ctx:
+        keep = ctx.enter_context(tc.tile_pool(name="keep", bufs=1))
+        psum = ctx.enter_context(tc.psum_pool(name="psum", bufs=BANKS))
+        ctx.enter_context(tc.manual_schedule())
+
+        x_raw = [keep.tile([P, 4, T], F32, name=f"x_raw{g}", align_bytes=256) for g in range(PASSES8)]
+        w_raw0 = keep.tile([P, 4, N], F32, name="w_raw0", align_bytes=256)
+        w_raw1 = [keep.tile([P, 4, w], F32, name=f"w_raw1_{h}", align_bytes=256) for h, w in enumerate((HEAD, N - HEAD))]
+        x4_w = keep.tile([P, PASSES4, 2 * T], U8, name="x4_w", align_bytes=256)
+        w4_w = keep.tile([P, PASSES4, 2 * N], U8, name="w4_w", align_bytes=256)
+        x4_s = keep.tile([P, PASSES4, T], U8, name="x4_s", align_bytes=256)
+        w4_s = keep.tile([P, PASSES4, N], U8, name="w4_s", align_bytes=256)
+        r_sb = [keep.tile([P, GROUP, T], F32, name=f"r_sb{h}", align_bytes=256) for h in range(TILES // GROUP)]
+        x_grp = [keep.tile([P, T, 4], BF16, name=f"x_grp{g}", align_bytes=256) for g in range(PASSES8)]
+        w_grp = [keep.tile([P, N, 4], BF16, name=f"w_grp{g}", align_bytes=256) for g in range(PASSES8)]
+        x_q = [keep.tile([P, T], U32, name=f"x_q{g}", align_bytes=256) for g in range(PASSES8)]
+        x_s = [keep.tile([P, T], U8, name=f"x_s{g}", align_bytes=256) for g in range(PASSES8)]
+        w_q = [keep.tile([P, N], U32, name=f"w_q{g}", align_bytes=256) for g in range(PASSES8)]
+        w_s = [keep.tile([P, N], U8, name=f"w_s{g}", align_bytes=256) for g in range(PASSES8)]
+        o_sb = [keep.tile([P, GROUP, T], F32, name=f"o_sb{h}", align_bytes=256) for h in range(TILES // GROUP)]
+
+        x8_v = x8.rearrange("(g p j) t -> g p j t", g=PASSES8, j=4)
+        w8_v = w8.rearrange("(g p j) n -> g p j n", g=PASSES8, j=4)
+        r_v = r.rearrange("(h i p) t -> h p i t", i=GROUP, p=P)
+        out_v = out.rearrange("(h i p) t -> h p i t", i=GROUP, p=P)
+        x4_scale_rows = x4_scales.bitcast(I32).rearrange("a (q s) t -> s q a t", s=4)
+        w4_scale_rows = w4_scales.bitcast(I32).rearrange("a (q s) n -> s q a n", s=4)
+
+        nc.sync.dma_start(out=x_raw[0][:], in_=x8_v[0])
+        nc.sync.dma_start(out=x_raw[1][:], in_=x8_v[1])
+
+        nc.vector.memset(x4_s[:].bitcast(I32), 0)
+        nc.vector.memset(w4_s[:].bitcast(I32), 0)
+        for s in range(4):
+            nc.sync.dma_start(out=x4_s[s:P:32, :, :].bitcast(I32), in_=x4_scale_rows[s])
+        nc.sync.dma_start(out=x4_w[:].bitcast(I32), in_=x4_words.bitcast(I32).rearrange("a p b -> p a b"))
+        nc.sync.dma_start(out=w4_w[:].bitcast(I32), in_=w4_words.bitcast(I32).rearrange("a p b -> p a b"))
+        for s in range(4):
+            nc.sync.dma_start(out=w4_s[s:P:32, :, :].bitcast(I32), in_=w4_scale_rows[s])
+        nc.sync.dma_start(out=w_raw0[:], in_=w8_v[0])
+        nc.sync.dma_start(out=w_raw1[0][:], in_=w8_v[1][:, :, 0:HEAD])
+        nc.sync.dma_start(out=r_sb[0][:], in_=r_v[0])
+        nc.sync.dma_start(out=r_sb[1][:], in_=r_v[1])
+        nc.sync.dma_start(out=w_raw1[1][:], in_=w8_v[1][:, :, HEAD:N])
+        nc.sync.dma_start(out=r_sb[2][:], in_=r_v[2])
+
+        for g in range(PASSES8):
+            lo, hi = slice(0, T // 2), slice(T // 2, T)
+            nc.vector.tensor_copy(out=x_grp[g][:, lo, :], in_=x_raw[g][:, :, lo].rearrange("p j t -> p t j"))
+            nc.scalar.copy(out=x_grp[g][:, hi, :], in_=x_raw[g][:, :, hi].rearrange("p j t -> p t j"))
+            nc.vector.quantize_mx(
+                out=x_q[g][:].bitcast(FP8X4), scales=x_s[g][:], in_=x_grp[g][:].rearrange("p t j -> p (t j)")
+            )
+
+        acc = {}
+
+        def cols(i):
+            return slice(i * P, (i + 1) * P)
+
+        def passes4(i):
+            acc[i] = psum.tile([P, T], F32, name="acc")
+            for a in range(PASSES4):
+                nc.tensor.matmul_mx(
+                    out=acc[i][:],
+                    lhsT=w4_w[:, a, 2 * i * P : 2 * (i + 1) * P].bitcast(FP4X4),
+                    lhsT_scale=w4_s[:, a, cols(i)],
+                    rhs=x4_w[:, a, :].bitcast(FP4X4),
+                    rhs_scale=x4_s[:, a, :],
+                    start=(a == 0),
+                    stop=False,
+                )
+
+        def pass8(g, i):
+            nc.tensor.matmul_mx(
+                out=acc[i][:],
+                lhsT=w_q[g][:, cols(i)].bitcast(FP8X4),
+                lhsT_scale=w_s[g][:, cols(i)],
+                rhs=x_q[g][:].bitcast(FP8X4),
+                rhs_scale=x_s[g][:],
+                start=False,
+                stop=(g == PASSES8 - 1),
+            )
+
+        def cast(g, i):
+            if g == 0:
+                src = w_raw0[:, :, cols(i)]
+            elif i < BANKS:
+                src = w_raw1[0][:, :, cols(i)]
+            else:
+                src = w_raw1[1][:, :, cols(i - BANKS)]
+            dst = w_grp[g][:, cols(i), :]
+            src = src.rearrange("p j n -> p n j")
+            if i % 2 == 0:
+                nc.vector.tensor_copy(out=dst, in_=src)
+            else:
+                nc.scalar.copy(out=dst, in_=src)
+
+        def quant(g, i):
+            nc.vector.quantize_mx(
+                out=w_q[g][:, cols(i)].bitcast(FP8X4),
+                scales=w_s[g][:, cols(i)],
+                in_=w_grp[g][:, cols(i), :].rearrange("p n j -> p (n j)"),
+            )
+
+        def prepare(g, first, last):
+            for i in range(first, last, 2):
+                cast(g, i)
+                cast(g, i + 1)
+                if i > first:
+                    quant(g, i - 2)
+                    quant(g, i - 1)
+            quant(g, last - 2)
+            quant(g, last - 1)
+
+        def finish(i):
+            nc.vector.tensor_tensor(
+                out=o_sb[i // GROUP][:, i % GROUP, :], in0=acc[i][:], in1=r_sb[i // GROUP][:, i % GROUP, :], op=mybir.AluOpType.add
+            )
+            if i in STORE_AFTER:
+                h, first, last = STORE_AFTER[i]
+                nc.sync.dma_start(out=out_v[h][:, first:last, :], in_=o_sb[h][:, first:last, :])
+
+        for i in range(BANKS):
+            passes4(i)
+        prepare(0, 0, TILES)
+        for i in range(BANKS):
+            pass8(0, i)
+        prepare(1, 0, BANKS)
+        for i in range(BANKS):
+            pass8(1, i)
+        for i in range(BANKS):
+            finish(i)
+        for i in range(BANKS, TILES):
+            passes4(i)
+            pass8(0, i)
+        prepare(1, BANKS, TILES)
+        for i in range(BANKS, TILES):
+            pass8(1, i)
+        for i in range(BANKS, TILES):
+            finish(i)

@@ -21,7 +21,10 @@ TILES = N // P
 BANKS = 8
 GROUP = 4
 HEAD = BANKS * P
-STORE_AFTER = {3: (0, 0, 4), 7: (1, 0, 4), 9: (2, 0, 2), 10: (2, 2, 3), 11: (2, 3, 4)}
+GROUPS = TILES // GROUP
+WIDE = GROUP * P
+PAIR = 2
+STORES = {3: (0, 4), 7: (0, 4), 9: (0, 2), 10: (2, 3), 11: (3, 4)}
 
 FLOPS = 2 * N * T * (K8 + K4)
 
@@ -33,40 +36,50 @@ def tile_mix_atom_fm_res_kernel(tc, x8, w8, x4_words, x4_scales, w4_words, w4_sc
         psum = ctx.enter_context(tc.psum_pool(name="psum", bufs=BANKS))
         ctx.enter_context(tc.manual_schedule())
 
-        x_raw = [keep.tile([P, 4, T], F32, name=f"x_raw{g}", align_bytes=256) for g in range(PASSES8)]
-        w_raw0 = keep.tile([P, 4, N], F32, name="w_raw0", align_bytes=256)
-        w_raw1 = [keep.tile([P, 4, w], F32, name=f"w_raw1_{h}", align_bytes=256) for h, w in enumerate((HEAD, N - HEAD))]
-        x4_w = keep.tile([P, PASSES4, 2 * T], U8, name="x4_w", align_bytes=256)
-        w4_w = keep.tile([P, PASSES4, 2 * N], U8, name="w4_w", align_bytes=256)
-        x4_s = keep.tile([P, PASSES4, T], U8, name="x4_s", align_bytes=256)
-        w4_s = keep.tile([P, PASSES4, N], U8, name="w4_s", align_bytes=256)
-        r_sb = [keep.tile([P, GROUP, T], F32, name=f"r_sb{h}", align_bytes=256) for h in range(TILES // GROUP)]
-        x_grp = [keep.tile([P, T, 4], BF16, name=f"x_grp{g}", align_bytes=256) for g in range(PASSES8)]
-        w_grp = [keep.tile([P, N, 4], BF16, name=f"w_grp{g}", align_bytes=256) for g in range(PASSES8)]
-        x_q = [keep.tile([P, T], U32, name=f"x_q{g}", align_bytes=256) for g in range(PASSES8)]
-        x_s = [keep.tile([P, T], U8, name=f"x_s{g}", align_bytes=256) for g in range(PASSES8)]
-        w_q = [keep.tile([P, N], U32, name=f"w_q{g}", align_bytes=256) for g in range(PASSES8)]
-        w_s = [keep.tile([P, N], U8, name=f"w_s{g}", align_bytes=256) for g in range(PASSES8)]
-        o_sb = [keep.tile([P, GROUP, T], F32, name=f"o_sb{h}", align_bytes=256) for h in range(TILES // GROUP)]
+        def sbuf(name, shape, dtype):
+            return keep.tile(shape, dtype, name=name, align_bytes=256)
+
+        x_raw = [sbuf(f"x_raw{g}", [P, 4, T], F32) for g in range(PASSES8)]
+        w_raw0 = sbuf("w_raw0", [P, 4, N], F32)
+        w_raw1 = [sbuf(f"w_raw1_{u}", [P, 4, w], F32) for u, w in enumerate((HEAD, N - HEAD))]
+        x4_w = sbuf("x4_w", [P, PASSES4, 2 * T], U8)
+        w4_w = sbuf("w4_w", [P, PASSES4, 2 * N], U8)
+        x4_s = sbuf("x4_s", [P, PASSES4, T], U8)
+        w4_s = sbuf("w4_s", [P, PASSES4, N], U8)
+        w4_wp = [sbuf(f"w4_wp{h}", [P, PASSES4, 2 * WIDE], U8) for h in range(GROUPS)]
+        w4_sp = [sbuf(f"w4_sp{h}", [P, PASSES4, WIDE], U8) for h in range(GROUPS)]
+        r_sb = [sbuf(f"r_sb{h}", [P, GROUP, T], F32) for h in range(GROUPS)]
+        x_grp = [sbuf(f"x_grp{g}", [P, T, 4], BF16) for g in range(PASSES8)]
+        w_grp = [sbuf(f"w_grp{g}", [P, N, 4], BF16) for g in range(PASSES8)]
+        x_q = [sbuf(f"x_q{g}", [P, T], U32) for g in range(PASSES8)]
+        x_s = [sbuf(f"x_s{g}", [P, T], U8) for g in range(PASSES8)]
+        w_q = [sbuf(f"w_q{g}", [P, N], U32) for g in range(PASSES8)]
+        w_s = [sbuf(f"w_s{g}", [P, N], U8) for g in range(PASSES8)]
+        o_sb = [sbuf(f"o_sb{h}", [P, GROUP, T], F32) for h in range(GROUPS)]
+
+        def cols(i, count=1):
+            return slice(i * P, (i + count) * P)
+
+        def span(h):
+            return slice(h * WIDE, (h + 1) * WIDE)
 
         x8_v = x8.rearrange("(g p j) t -> g p j t", g=PASSES8, j=4)
         w8_v = w8.rearrange("(g p j) n -> g p j n", g=PASSES8, j=4)
-        r_v = r.rearrange("(h i p) t -> h p i t", i=GROUP, p=P)
-        out_v = out.rearrange("(h i p) t -> h p i t", i=GROUP, p=P)
+        r_v = r.rearrange("(h p i) t -> h p i t", i=GROUP, p=P)
+        out_v = out.rearrange("(h p i) t -> h p i t", i=GROUP, p=P)
         x4_scale_rows = x4_scales.bitcast(I32).rearrange("a (q s) t -> s q a t", s=4)
         w4_scale_rows = w4_scales.bitcast(I32).rearrange("a (q s) n -> s q a n", s=4)
 
-        nc.sync.dma_start(out=x_raw[0][:], in_=x8_v[0])
-        nc.sync.dma_start(out=x_raw[1][:], in_=x8_v[1])
-
+        nc.sync.dma_start(out=x4_w[:].bitcast(I32), in_=x4_words.bitcast(I32).rearrange("a p b -> p a b"))
         nc.vector.memset(x4_s[:].bitcast(I32), 0)
         nc.vector.memset(w4_s[:].bitcast(I32), 0)
         for s in range(4):
             nc.sync.dma_start(out=x4_s[s:P:32, :, :].bitcast(I32), in_=x4_scale_rows[s])
-        nc.sync.dma_start(out=x4_w[:].bitcast(I32), in_=x4_words.bitcast(I32).rearrange("a p b -> p a b"))
         nc.sync.dma_start(out=w4_w[:].bitcast(I32), in_=w4_words.bitcast(I32).rearrange("a p b -> p a b"))
         for s in range(4):
             nc.sync.dma_start(out=w4_s[s:P:32, :, :].bitcast(I32), in_=w4_scale_rows[s])
+        nc.sync.dma_start(out=x_raw[0][:], in_=x8_v[0])
+        nc.sync.dma_start(out=x_raw[1][:], in_=x8_v[1])
         nc.sync.dma_start(out=w_raw0[:], in_=w8_v[0])
         nc.sync.dma_start(out=w_raw1[0][:], in_=w8_v[1][:, :, 0:HEAD])
         nc.sync.dma_start(out=r_sb[0][:], in_=r_v[0])
@@ -74,26 +87,57 @@ def tile_mix_atom_fm_res_kernel(tc, x8, w8, x4_words, x4_scales, w4_words, w4_sc
         nc.sync.dma_start(out=w_raw1[1][:], in_=w8_v[1][:, :, HEAD:N])
         nc.sync.dma_start(out=r_sb[2][:], in_=r_v[2])
 
-        for g in range(PASSES8):
-            lo, hi = slice(0, T // 2), slice(T // 2, T)
-            nc.vector.tensor_copy(out=x_grp[g][:, lo, :], in_=x_raw[g][:, :, lo].rearrange("p j t -> p t j"))
-            nc.scalar.copy(out=x_grp[g][:, hi, :], in_=x_raw[g][:, :, hi].rearrange("p j t -> p t j"))
+        def copy(engine, dst, src):
+            if engine == "vector":
+                nc.vector.tensor_copy(out=dst, in_=src)
+            else:
+                nc.scalar.copy(out=dst, in_=src)
+
+        def prepare_x(g):
+            copy("scalar", x_grp[g][:], x_raw[g][:].rearrange("p j t -> p t j"))
             nc.vector.quantize_mx(
                 out=x_q[g][:].bitcast(FP8X4), scales=x_s[g][:], in_=x_grp[g][:].rearrange("p t j -> p (t j)")
             )
 
+        def permute(h):
+            nc.vector.tensor_copy(
+                out=w4_wp[h][:].rearrange("p a (i m b) -> p a i m b", i=GROUP, b=2),
+                in_=w4_w[:, :, 2 * h * WIDE : 2 * (h + 1) * WIDE].rearrange("p a (m i b) -> p a i m b", i=GROUP, b=2),
+            )
+            nc.vector.tensor_copy(
+                out=w4_sp[h][:].rearrange("p a (i m) -> p a i m", i=GROUP),
+                in_=w4_s[:, :, span(h)].rearrange("p a (m i) -> p a i m", i=GROUP),
+            )
+
+        def cast(g, h):
+            if g == 0:
+                raw = w_raw0[:, :, span(h)]
+            elif h < GROUPS - 1:
+                raw = w_raw1[0][:, :, span(h)]
+            else:
+                raw = w_raw1[1][:]
+            src = raw.rearrange("p j (m i) -> p m j i", i=GROUP)
+            dst = w_grp[g][:, span(h), :].rearrange("p (i m) j -> p m j i", i=GROUP)
+            copy("vector", dst[:, :, :, 0:PAIR], src[:, :, :, 0:PAIR])
+            copy("scalar", dst[:, :, :, PAIR:GROUP], src[:, :, :, PAIR:GROUP])
+
+        def quant(g, i):
+            nc.vector.quantize_mx(
+                out=w_q[g][:, cols(i, PAIR)].bitcast(FP8X4),
+                scales=w_s[g][:, cols(i, PAIR)],
+                in_=w_grp[g][:, cols(i, PAIR), :].rearrange("p n j -> p (n j)"),
+            )
+
         acc = {}
 
-        def cols(i):
-            return slice(i * P, (i + 1) * P)
-
         def passes4(i):
+            h, c = divmod(i, GROUP)
             acc[i] = psum.tile([P, T], F32, name="acc")
             for a in range(PASSES4):
                 nc.tensor.matmul_mx(
                     out=acc[i][:],
-                    lhsT=w4_w[:, a, 2 * i * P : 2 * (i + 1) * P].bitcast(FP4X4),
-                    lhsT_scale=w4_s[:, a, cols(i)],
+                    lhsT=w4_wp[h][:, a, 2 * c * P : 2 * (c + 1) * P].bitcast(FP4X4),
+                    lhsT_scale=w4_sp[h][:, a, cols(c)],
                     rhs=x4_w[:, a, :].bitcast(FP4X4),
                     rhs_scale=x4_s[:, a, :],
                     start=(a == 0),
@@ -111,51 +155,30 @@ def tile_mix_atom_fm_res_kernel(tc, x8, w8, x4_words, x4_scales, w4_words, w4_sc
                 stop=(g == PASSES8 - 1),
             )
 
-        def cast(g, i):
-            if g == 0:
-                src = w_raw0[:, :, cols(i)]
-            elif i < BANKS:
-                src = w_raw1[0][:, :, cols(i)]
-            else:
-                src = w_raw1[1][:, :, cols(i - BANKS)]
-            dst = w_grp[g][:, cols(i), :]
-            src = src.rearrange("p j n -> p n j")
-            if i % 2 == 0:
-                nc.vector.tensor_copy(out=dst, in_=src)
-            else:
-                nc.scalar.copy(out=dst, in_=src)
-
-        def quant(g, i):
-            nc.vector.quantize_mx(
-                out=w_q[g][:, cols(i)].bitcast(FP8X4),
-                scales=w_s[g][:, cols(i)],
-                in_=w_grp[g][:, cols(i), :].rearrange("p n j -> p (n j)"),
-            )
-
-        def prepare(g, first, last):
-            for i in range(first, last, 2):
-                cast(g, i)
-                cast(g, i + 1)
-                if i > first:
-                    quant(g, i - 2)
-                    quant(g, i - 1)
-            quant(g, last - 2)
-            quant(g, last - 1)
-
         def finish(i):
-            nc.vector.tensor_tensor(
-                out=o_sb[i // GROUP][:, i % GROUP, :], in0=acc[i][:], in1=r_sb[i // GROUP][:, i % GROUP, :], op=mybir.AluOpType.add
-            )
-            if i in STORE_AFTER:
-                h, first, last = STORE_AFTER[i]
+            h, c = divmod(i, GROUP)
+            nc.vector.tensor_tensor(out=o_sb[h][:, c, :], in0=acc[i][:], in1=r_sb[h][:, c, :], op=mybir.AluOpType.add)
+            if i in STORES:
+                first, last = STORES[i]
                 nc.sync.dma_start(out=out_v[h][:, first:last, :], in_=o_sb[h][:, first:last, :])
 
+        permute(0)
+        permute(1)
         for i in range(BANKS):
             passes4(i)
-        prepare(0, 0, TILES)
+        prepare_x(0)
+        permute(2)
+        prepare_x(1)
+        for h in range(GROUPS):
+            cast(0, h)
+        for i in range(0, TILES, PAIR):
+            quant(0, i)
         for i in range(BANKS):
             pass8(0, i)
-        prepare(1, 0, BANKS)
+        for h in range(GROUPS - 1):
+            cast(1, h)
+        for i in range(0, BANKS, PAIR):
+            quant(1, i)
         for i in range(BANKS):
             pass8(1, i)
         for i in range(BANKS):
@@ -163,7 +186,9 @@ def tile_mix_atom_fm_res_kernel(tc, x8, w8, x4_words, x4_scales, w4_words, w4_sc
         for i in range(BANKS, TILES):
             passes4(i)
             pass8(0, i)
-        prepare(1, BANKS, TILES)
+        cast(1, GROUPS - 1)
+        for i in range(BANKS, TILES, PAIR):
+            quant(1, i)
         for i in range(BANKS, TILES):
             pass8(1, i)
         for i in range(BANKS, TILES):

@@ -5,6 +5,7 @@ import concourse.mybir as mybir
 F32 = mybir.dt.float32
 BF16 = mybir.dt.bfloat16
 U32 = mybir.dt.uint32
+U16 = mybir.dt.uint16
 U8 = mybir.dt.uint8
 I32 = mybir.dt.int32
 FP8X4 = mybir.dt.float8_e4m3fn_x4
@@ -79,8 +80,8 @@ def tile_mix_atom_fm_res_kernel(tc, x8, w8, x4_words, x4_scales, w4_words, w4_sc
         for s in range(4):
             nc.sync.dma_start(out=w4_s[s:P:32, :, :].bitcast(I32), in_=w4_scale_rows[s])
         nc.sync.dma_start(out=x_raw[0][:], in_=x8_v[0])
-        nc.sync.dma_start(out=x_raw[1][:], in_=x8_v[1])
         nc.sync.dma_start(out=w_raw0[:], in_=w8_v[0])
+        nc.sync.dma_start(out=x_raw[1][:], in_=x8_v[1])
         nc.sync.dma_start(out=w_raw1[0][:], in_=w8_v[1][:, :, 0:HEAD])
         nc.sync.dma_start(out=r_sb[0][:], in_=r_v[0])
         nc.sync.dma_start(out=r_sb[1][:], in_=r_v[1])
@@ -93,23 +94,26 @@ def tile_mix_atom_fm_res_kernel(tc, x8, w8, x4_words, x4_scales, w4_words, w4_sc
             else:
                 nc.scalar.copy(out=dst, in_=src)
 
-        def prepare_x(g):
-            copy("scalar", x_grp[g][:], x_raw[g][:].rearrange("p j t -> p t j"))
+        def cast_x(g, engine):
+            copy(engine, x_grp[g][:], x_raw[g][:].rearrange("p j t -> p t j"))
+
+        def quant_x(g):
             nc.vector.quantize_mx(
                 out=x_q[g][:].bitcast(FP8X4), scales=x_s[g][:], in_=x_grp[g][:].rearrange("p t j -> p (t j)")
             )
 
         def permute(h):
             nc.vector.tensor_copy(
-                out=w4_wp[h][:].rearrange("p a (i m b) -> p a i m b", i=GROUP, b=2),
-                in_=w4_w[:, :, 2 * h * WIDE : 2 * (h + 1) * WIDE].rearrange("p a (m i b) -> p a i m b", i=GROUP, b=2),
+                out=w4_wp[h][:].bitcast(U16).rearrange("p a (i m) -> p a i m", i=GROUP),
+                in_=w4_w[:].bitcast(U16)[:, :, span(h)].rearrange("p a (m i) -> p a i m", i=GROUP),
             )
             nc.vector.tensor_copy(
                 out=w4_sp[h][:].rearrange("p a (i m) -> p a i m", i=GROUP),
                 in_=w4_s[:, :, span(h)].rearrange("p a (m i) -> p a i m", i=GROUP),
             )
 
-        def cast(g, h):
+        def cast(g, i, engine):
+            h, c = divmod(i, GROUP)
             if g == 0:
                 raw = w_raw0[:, :, span(h)]
             elif h < GROUPS - 1:
@@ -118,8 +122,7 @@ def tile_mix_atom_fm_res_kernel(tc, x8, w8, x4_words, x4_scales, w4_words, w4_sc
                 raw = w_raw1[1][:]
             src = raw.rearrange("p j (m i) -> p m j i", i=GROUP)
             dst = w_grp[g][:, span(h), :].rearrange("p (i m) j -> p m j i", i=GROUP)
-            copy("vector", dst[:, :, :, 0:PAIR], src[:, :, :, 0:PAIR])
-            copy("scalar", dst[:, :, :, PAIR:GROUP], src[:, :, :, PAIR:GROUP])
+            copy(engine, dst[:, :, :, c : c + PAIR], src[:, :, :, c : c + PAIR])
 
         def quant(g, i):
             nc.vector.quantize_mx(
@@ -162,34 +165,67 @@ def tile_mix_atom_fm_res_kernel(tc, x8, w8, x4_words, x4_scales, w4_words, w4_sc
                 first, last = STORES[i]
                 nc.sync.dma_start(out=out_v[h][:, first:last, :], in_=o_sb[h][:, first:last, :])
 
+        def close(*tiles):
+            for i in tiles:
+                pass8(1, i)
+
+        def open_late(i):
+            passes4(i)
+            pass8(0, i)
+
         permute(0)
         permute(1)
-        for i in range(BANKS):
+        for i in range(BANKS - 3):
             passes4(i)
-        prepare_x(0)
+        cast_x(0, "scalar")
         permute(2)
-        prepare_x(1)
-        for h in range(GROUPS):
-            cast(0, h)
-        for i in range(0, TILES, PAIR):
+        quant_x(0)
+
+        cast(0, 0, "vector")
+        cast(0, 2, "scalar")
+        cast(0, 6, "scalar")
+        cast(0, 10, "scalar")
+        cast(0, 4, "vector")
+        quant(0, 0)
+        cast(0, 8, "vector")
+        for i in (4, 2, 8):
             quant(0, i)
-        for i in range(BANKS):
-            pass8(0, i)
-        for h in range(GROUPS - 1):
-            cast(1, h)
-        for i in range(0, BANKS, PAIR):
+        cast_x(1, "vector")
+        quant(0, 6)
+        quant_x(1)
+        quant(0, 10)
+        for held, pair in ((5, 0), (6, 4), (7, 2)):
+            pass8(0, pair)
+            passes4(held)
+            pass8(0, pair + 1)
+        pass8(0, 6)
+        pass8(0, 7)
+
+        cast(1, 0, "vector")
+        cast(1, 2, "scalar")
+        cast(1, 6, "scalar")
+        cast(1, 4, "vector")
+        for i in (0, 4, 2):
             quant(1, i)
-        for i in range(BANKS):
-            pass8(1, i)
-        for i in range(BANKS):
+        close(0, 1, 4, 5, 2, 3)
+        finish(0)
+        finish(1)
+        open_late(8)
+        quant(1, 6)
+        close(6, 7)
+        for i in range(2, BANKS - 1):
             finish(i)
-        for i in range(BANKS, TILES):
-            passes4(i)
-            pass8(0, i)
-        cast(1, GROUPS - 1)
-        for i in range(BANKS, TILES, PAIR):
-            quant(1, i)
-        for i in range(BANKS, TILES):
-            pass8(1, i)
+        cast(1, 10, "scalar")
+        cast(1, 8, "vector")
+        finish(BANKS - 1)
+        open_late(9)
+        open_late(10)
+        quant(1, 8)
+        quant(1, 10)
+        close(8, 9)
+        passes4(11)
+        close(10)
+        pass8(0, 11)
+        close(11)
         for i in range(BANKS, TILES):
             finish(i)

@@ -75,10 +75,12 @@ def tile_mix_atom_fm_res_kernel(tc, x8, w8, x4_words, x4_scales, w4_words, w4_sc
         nc.vector.memset(x4_s[:].bitcast(I32), 0)
         nc.vector.memset(w4_s[:].bitcast(I32), 0)
         for s in range(4):
-            nc.sync.dma_start(out=x4_s[s:P:32, :, :].bitcast(I32), in_=x4_scale_rows[s])
+            queue = nc.sync if s == 0 else nc.scalar
+            queue.dma_start(out=x4_s[s:P:32, :, :].bitcast(I32), in_=x4_scale_rows[s])
         nc.sync.dma_start(out=w4_w[:].bitcast(I32), in_=w4_words.bitcast(I32).rearrange("a p b -> p a b"))
         for s in range(4):
-            nc.sync.dma_start(out=w4_s[s:P:32, :, :].bitcast(I32), in_=w4_scale_rows[s])
+            queue = nc.sync if s == 0 else nc.scalar
+            queue.dma_start(out=w4_s[s:P:32, :, :].bitcast(I32), in_=w4_scale_rows[s])
         nc.sync.dma_start(out=x_raw[0][:], in_=x8_v[0])
         nc.sync.dma_start(out=w_raw0[:], in_=w8_v[0])
         nc.sync.dma_start(out=x_raw[1][:], in_=x8_v[1])

@@ -10,6 +10,7 @@ U8 = mybir.dt.uint8
 I32 = mybir.dt.int32
 FP8X4 = mybir.dt.float8_e4m3fn_x4
 FP4X4 = mybir.dt.float4_e2m1fn_x4
+ADD = mybir.AluOpType.add
 
 P = 128
 T = 512
@@ -19,13 +20,13 @@ K4 = 2048
 PASSES8 = K8 // 512
 PASSES4 = K4 // 512
 TILES = N // P
-BANKS = 8
-GROUP = 4
-HEAD = BANKS * P
-GROUPS = TILES // GROUP
-WIDE = GROUP * P
+QUAD = 4
+FRONT = QUAD * P
+CUT = 3 * N + FRONT
 PAIR = 2
-STORES = {3: (0, 4), 7: (0, 4), 9: (0, 2), 10: (2, 3), 11: (3, 4)}
+PARKED = 6
+R_LOADS = ((0, 2), (2, 4), (4, 7), (7, 12))
+STORES = ((0, 4), (4, 7), (7, 9), (9, 11), (11, 12))
 
 FLOPS = 2 * N * T * (K8 + K4)
 
@@ -34,40 +35,51 @@ def tile_mix_atom_fm_res_kernel(tc, x8, w8, x4_words, x4_scales, w4_words, w4_sc
     nc = tc.nc
     with ExitStack() as ctx:
         keep = ctx.enter_context(tc.tile_pool(name="keep", bufs=1))
-        psum = ctx.enter_context(tc.psum_pool(name="psum", bufs=BANKS))
+        psum = ctx.enter_context(tc.psum_pool(name="psum", bufs=1))
         ctx.enter_context(tc.manual_schedule())
 
         def sbuf(name, shape, dtype):
             return keep.tile(shape, dtype, name=name, align_bytes=256)
 
         x_raw = [sbuf(f"x_raw{g}", [P, 4, T], F32) for g in range(PASSES8)]
-        w_raw0 = sbuf("w_raw0", [P, 4, N], F32)
-        w_raw1 = [sbuf(f"w_raw1_{u}", [P, 4, w], F32) for u, w in enumerate((HEAD, N - HEAD))]
+        w_raw = [sbuf(f"w_raw{g}", [P, 4, N], F32) for g in range(PASSES8)]
         x4_w = sbuf("x4_w", [P, PASSES4, 2 * T], U8)
         w4_w = sbuf("w4_w", [P, PASSES4, 2 * N], U8)
         x4_s = sbuf("x4_s", [P, PASSES4, T], U8)
         w4_s = sbuf("w4_s", [P, PASSES4, N], U8)
-        w4_wp = [sbuf(f"w4_wp{h}", [P, PASSES4, 2 * WIDE], U8) for h in range(GROUPS)]
-        w4_sp = [sbuf(f"w4_sp{h}", [P, PASSES4, WIDE], U8) for h in range(GROUPS)]
-        r_sb = [sbuf(f"r_sb{h}", [P, GROUP, T], F32) for h in range(GROUPS)]
+        w4_wp = [sbuf(f"w4_wp{h}", [P, PASSES4, 2 * QUAD * P], U8) for h in range(TILES // QUAD)]
+        w4_sp = [sbuf(f"w4_sp{h}", [P, PASSES4, QUAD * P], U8) for h in range(TILES // QUAD)]
+        r_sb = [sbuf(f"r_sb{first}", [P, last - first, T], F32) for first, last in R_LOADS]
         x_grp = [sbuf(f"x_grp{g}", [P, T, 4], BF16) for g in range(PASSES8)]
         w_grp = [sbuf(f"w_grp{g}", [P, N, 4], BF16) for g in range(PASSES8)]
         x_q = [sbuf(f"x_q{g}", [P, T], U32) for g in range(PASSES8)]
         x_s = [sbuf(f"x_s{g}", [P, T], U8) for g in range(PASSES8)]
         w_q = [sbuf(f"w_q{g}", [P, N], U32) for g in range(PASSES8)]
         w_s = [sbuf(f"w_s{g}", [P, N], U8) for g in range(PASSES8)]
-        o_sb = [sbuf(f"o_sb{h}", [P, GROUP, T], F32) for h in range(GROUPS)]
+        parked = sbuf("parked", [P, T], F32)
+        o_sb = sbuf("o_sb", [P, TILES, T], F32)
 
         def cols(i, count=1):
             return slice(i * P, (i + count) * P)
 
-        def span(h):
-            return slice(h * WIDE, (h + 1) * WIDE)
+        def r_of(i):
+            u = [last > i for first, last in R_LOADS].index(True)
+            return r_sb[u][:, i - R_LOADS[u][0], :]
 
         x8_v = x8.rearrange("(g p j) t -> g p j t", g=PASSES8, j=4)
         w8_v = w8.rearrange("(g p j) n -> g p j n", g=PASSES8, j=4)
-        r_v = r.rearrange("(h p i) t -> h p i t", i=GROUP, p=P)
-        out_v = out.rearrange("(h p i) t -> h p i t", i=GROUP, p=P)
+
+        def rows_of(dram, first, last):
+            if first < QUAD:
+                return dram[0:FRONT, :].rearrange("(p c) t -> p c t", p=P)[:, first:last, :]
+            return dram[FRONT:N, :].rearrange("(p c) t -> p c t", p=P)[:, first - QUAD : last - QUAD, :]
+
+        def columns_of(view, first, count):
+            if first < QUAD:
+                return view[:, :, 0:FRONT].rearrange("p a (m c) -> p a m c", m=P)[:, :, :, first : first + count]
+            back = view[:, :, FRONT:N].rearrange("p a (m c) -> p a m c", m=P)
+            return back[:, :, :, first - QUAD : first - QUAD + count]
+
         x4_scale_rows = x4_scales.bitcast(I32).rearrange("a (q s) t -> s q a t", s=4)
         w4_scale_rows = w4_scales.bitcast(I32).rearrange("a (q s) n -> s q a n", s=4)
 
@@ -82,13 +94,15 @@ def tile_mix_atom_fm_res_kernel(tc, x8, w8, x4_words, x4_scales, w4_words, w4_sc
             queue = nc.sync if s == 0 else nc.scalar
             queue.dma_start(out=w4_s[s:P:32, :, :].bitcast(I32), in_=w4_scale_rows[s])
         nc.sync.dma_start(out=x_raw[0][:], in_=x8_v[0])
-        nc.sync.dma_start(out=w_raw0[:], in_=w8_v[0])
+        nc.sync.dma_start(out=w_raw[0][:], in_=w8_v[0])
         nc.sync.dma_start(out=x_raw[1][:], in_=x8_v[1])
-        nc.sync.dma_start(out=w_raw1[0][:], in_=w8_v[1][:, :, 0:HEAD])
-        nc.sync.dma_start(out=r_sb[0][:], in_=r_v[0])
-        nc.sync.dma_start(out=r_sb[1][:], in_=r_v[1])
-        nc.sync.dma_start(out=w_raw1[1][:], in_=w8_v[1][:, :, HEAD:N])
-        nc.sync.dma_start(out=r_sb[2][:], in_=r_v[2])
+        w_run = w_raw[1][:].rearrange("p j n -> p (j n)")
+        w8_run = w8_v[1].rearrange("p j n -> p (j n)")
+        nc.sync.dma_start(out=w_run[:, 0:CUT], in_=w8_run[:, 0:CUT])
+        for u, (first, last) in enumerate(R_LOADS):
+            nc.sync.dma_start(out=r_sb[u][:], in_=rows_of(r, first, last))
+            if u == 0:
+                nc.sync.dma_start(out=w_run[:, CUT:], in_=w8_run[:, CUT:])
 
         def copy(engine, dst, src):
             if engine == "vector":
@@ -106,38 +120,34 @@ def tile_mix_atom_fm_res_kernel(tc, x8, w8, x4_words, x4_scales, w4_words, w4_sc
 
         def permute(h):
             nc.vector.tensor_copy(
-                out=w4_wp[h][:].bitcast(U16).rearrange("p a (i m) -> p a i m", i=GROUP),
-                in_=w4_w[:].bitcast(U16)[:, :, span(h)].rearrange("p a (m i) -> p a i m", i=GROUP),
+                out=w4_wp[h][:].bitcast(U16).rearrange("p a (i m) -> p a m i", i=QUAD),
+                in_=columns_of(w4_w[:].bitcast(U16), h * QUAD, QUAD),
             )
             nc.vector.tensor_copy(
-                out=w4_sp[h][:].rearrange("p a (i m) -> p a i m", i=GROUP),
-                in_=w4_s[:, :, span(h)].rearrange("p a (m i) -> p a i m", i=GROUP),
+                out=w4_sp[h][:].rearrange("p a (i m) -> p a m i", i=QUAD),
+                in_=columns_of(w4_s[:], h * QUAD, QUAD),
             )
 
-        def cast(g, i, engine):
-            h, c = divmod(i, GROUP)
-            if g == 0:
-                raw = w_raw0[:, :, span(h)]
-            elif h < GROUPS - 1:
-                raw = w_raw1[0][:, :, span(h)]
-            else:
-                raw = w_raw1[1][:]
-            src = raw.rearrange("p j (m i) -> p m j i", i=GROUP)
-            dst = w_grp[g][:, span(h), :].rearrange("p (i m) j -> p m j i", i=GROUP)
-            copy(engine, dst[:, :, :, c : c + PAIR], src[:, :, :, c : c + PAIR])
+        def cast(g, i, engine, count=PAIR):
+            src = columns_of(w_raw[g][:], i, count).rearrange("p j m c -> p m j c")
+            dst = w_grp[g][:].rearrange("p (c m) j -> p m j c", c=TILES)
+            copy(engine, dst[:, :, :, i : i + count], src)
 
-        def quant(g, i):
+        def quant(g, i, count=PAIR):
             nc.vector.quantize_mx(
-                out=w_q[g][:, cols(i, PAIR)].bitcast(FP8X4),
-                scales=w_s[g][:, cols(i, PAIR)],
-                in_=w_grp[g][:, cols(i, PAIR), :].rearrange("p n j -> p (n j)"),
+                out=w_q[g][:, cols(i, count)].bitcast(FP8X4),
+                scales=w_s[g][:, cols(i, count)],
+                in_=w_grp[g][:, cols(i, count), :].rearrange("p n j -> p (n j)"),
             )
 
         acc = {}
 
-        def passes4(i):
-            h, c = divmod(i, GROUP)
-            acc[i] = psum.tile([P, T], F32, name="acc")
+        def take_bank(i, bank):
+            acc[i] = psum.tile([P, T], F32, name=f"bank{bank}")
+
+        def passes4(i, bank):
+            h, c = divmod(i, QUAD)
+            take_bank(i, bank)
             for a in range(PASSES4):
                 nc.tensor.matmul_mx(
                     out=acc[i][:],
@@ -149,85 +159,88 @@ def tile_mix_atom_fm_res_kernel(tc, x8, w8, x4_words, x4_scales, w4_words, w4_sc
                     stop=False,
                 )
 
-        def pass8(g, i):
+        def pass8(g, i, start=False, stop=False):
             nc.tensor.matmul_mx(
                 out=acc[i][:],
                 lhsT=w_q[g][:, cols(i)].bitcast(FP8X4),
                 lhsT_scale=w_s[g][:, cols(i)],
                 rhs=x_q[g][:].bitcast(FP8X4),
                 rhs_scale=x_s[g][:],
-                start=False,
-                stop=(g == PASSES8 - 1),
+                start=start,
+                stop=stop,
             )
 
         def finish(i):
-            h, c = divmod(i, GROUP)
-            nc.vector.tensor_tensor(out=o_sb[h][:, c, :], in0=acc[i][:], in1=r_sb[h][:, c, :], op=mybir.AluOpType.add)
-            if i in STORES:
-                first, last = STORES[i]
-                nc.sync.dma_start(out=out_v[h][:, first:last, :], in_=o_sb[h][:, first:last, :])
+            other = parked[:] if i == PARKED else r_of(i)
+            nc.vector.tensor_tensor(out=o_sb[:, i, :], in0=acc[i][:], in1=other, op=ADD)
+            for first, last in STORES:
+                if i == last - 1:
+                    nc.sync.dma_start(out=rows_of(out, first, last), in_=o_sb[:, first:last, :])
 
         def close(*tiles):
             for i in tiles:
-                pass8(1, i)
+                pass8(1, i, stop=True)
 
-        def open_late(i):
-            passes4(i)
+        def open_late(i, bank):
+            passes4(i, bank)
             pass8(0, i)
 
-        permute(0)
         permute(1)
-        for i in range(BANKS - 3):
-            passes4(i)
+        permute(0)
+        for i in (6, 7, 4, 5, 0):
+            passes4(i, i)
         cast_x(0, "scalar")
         permute(2)
         quant_x(0)
 
-        cast(0, 0, "vector")
-        cast(0, 2, "scalar")
-        cast(0, 6, "scalar")
-        cast(0, 10, "scalar")
+        cast(0, 6, "vector")
+        cast(0, 0, "scalar")
         cast(0, 4, "vector")
-        quant(0, 0)
+        quant(0, 6)
+        pass8(0, PARKED, stop=True)
+        nc.scalar.copy(out=parked[:], in_=acc[PARKED][:])
+        cast(0, 2, "scalar")
+        cast(0, 10, "scalar")
         cast(0, 8, "vector")
-        for i in (4, 2, 8):
+        for i in (4, 0, 8):
             quant(0, i)
         cast_x(1, "vector")
-        quant(0, 6)
+        quant(0, 2)
         quant_x(1)
         quant(0, 10)
-        for held, pair in ((5, 0), (6, 4), (7, 2)):
-            pass8(0, pair)
-            passes4(held)
-            pass8(0, pair + 1)
-        pass8(0, 6)
         pass8(0, 7)
+        for i in (1, 2, 3):
+            passes4(i, i)
+        for i in (4, 5, 0, 1, 2, 3):
+            pass8(0, i)
+        open_late(8, PARKED)
 
         cast(1, 0, "vector")
-        cast(1, 2, "scalar")
-        cast(1, 6, "scalar")
-        cast(1, 4, "vector")
-        for i in (0, 4, 2):
-            quant(1, i)
-        close(0, 1, 4, 5, 2, 3)
+        for i in range(2, TILES, PAIR):
+            cast(1, i, "scalar")
+        quant(1, 0)
+        quant(1, 2)
+        close(0, 1, 2, 3)
         finish(0)
         finish(1)
-        open_late(8)
+        open_late(9, 0)
+        finish(2)
+        quant(1, 4)
+        close(4, 5)
+        open_late(10, 1)
+        finish(3)
         quant(1, 6)
-        close(6, 7)
-        for i in range(2, BANKS - 1):
-            finish(i)
-        cast(1, 10, "scalar")
-        cast(1, 8, "vector")
-        finish(BANKS - 1)
-        open_late(9)
-        open_late(10)
+        take_bank(PARKED, 2)
+        pass8(1, PARKED, start=True, stop=True)
+        close(7)
+        finish(4)
+        nc.vector.tensor_tensor(out=parked[:], in0=parked[:], in1=r_of(PARKED), op=ADD)
+        finish(5)
+        open_late(11, 3)
+        finish(6)
         quant(1, 8)
-        quant(1, 10)
         close(8, 9)
-        passes4(11)
-        close(10)
-        pass8(0, 11)
-        close(11)
-        for i in range(BANKS, TILES):
+        quant(1, 10)
+        close(10, 11)
+        for i in range(7, TILES):
             finish(i)

from contextlib import ExitStack

import concourse.mybir as mybir

F32 = mybir.dt.float32
BF16 = mybir.dt.bfloat16
U32 = mybir.dt.uint32
U16 = mybir.dt.uint16
U8 = mybir.dt.uint8
I32 = mybir.dt.int32
FP8X4 = mybir.dt.float8_e4m3fn_x4
FP4X4 = mybir.dt.float4_e2m1fn_x4
ADD = mybir.AluOpType.add

P = 128
T = 512
N = 1536
K8 = 1024
K4 = 2048
PASSES8 = K8 // 512
PASSES4 = K4 // 512
TILES = N // P
QUAD = 4
FRONT = QUAD * P
CUT = 3 * N + FRONT
PAIR = 2
PARKED = 6
R_LOADS = ((0, 2), (2, 4), (4, 7), (7, 12))
STORES = ((0, 4), (4, 7), (7, 9), (9, 11), (11, 12))

FLOPS = 2 * N * T * (K8 + K4)


def tile_mix_atom_fm_res_kernel(tc, x8, w8, x4_words, x4_scales, w4_words, w4_scales, r, out):
    nc = tc.nc
    with ExitStack() as ctx:
        keep = ctx.enter_context(tc.tile_pool(name="keep", bufs=1))
        psum = ctx.enter_context(tc.psum_pool(name="psum", bufs=1))
        ctx.enter_context(tc.manual_schedule())

        def sbuf(name, shape, dtype):
            return keep.tile(shape, dtype, name=name, align_bytes=256)

        x_raw = [sbuf(f"x_raw{g}", [P, 4, T], F32) for g in range(PASSES8)]
        w_raw = [sbuf(f"w_raw{g}", [P, 4, N], F32) for g in range(PASSES8)]
        x4_w = sbuf("x4_w", [P, PASSES4, 2 * T], U8)
        w4_w = sbuf("w4_w", [P, PASSES4, 2 * N], U8)
        x4_s = sbuf("x4_s", [P, PASSES4, T], U8)
        w4_s = sbuf("w4_s", [P, PASSES4, N], U8)
        w4_wp = [sbuf(f"w4_wp{h}", [P, PASSES4, 2 * QUAD * P], U8) for h in range(TILES // QUAD)]
        w4_sp = [sbuf(f"w4_sp{h}", [P, PASSES4, QUAD * P], U8) for h in range(TILES // QUAD)]
        r_sb = [sbuf(f"r_sb{first}", [P, last - first, T], F32) for first, last in R_LOADS]
        x_grp = [sbuf(f"x_grp{g}", [P, T, 4], BF16) for g in range(PASSES8)]
        w_grp = [sbuf(f"w_grp{g}", [P, N, 4], BF16) for g in range(PASSES8)]
        x_q = [sbuf(f"x_q{g}", [P, T], U32) for g in range(PASSES8)]
        x_s = [sbuf(f"x_s{g}", [P, T], U8) for g in range(PASSES8)]
        w_q = [sbuf(f"w_q{g}", [P, N], U32) for g in range(PASSES8)]
        w_s = [sbuf(f"w_s{g}", [P, N], U8) for g in range(PASSES8)]
        parked = sbuf("parked", [P, T], F32)
        o_sb = sbuf("o_sb", [P, TILES, T], F32)

        def cols(i, count=1):
            return slice(i * P, (i + count) * P)

        def r_of(i):
            u = [last > i for first, last in R_LOADS].index(True)
            return r_sb[u][:, i - R_LOADS[u][0], :]

        x8_v = x8.rearrange("(g p j) t -> g p j t", g=PASSES8, j=4)
        w8_v = w8.rearrange("(g p j) n -> g p j n", g=PASSES8, j=4)

        def rows_of(dram, first, last):
            if first < QUAD:
                return dram[0:FRONT, :].rearrange("(p c) t -> p c t", p=P)[:, first:last, :]
            return dram[FRONT:N, :].rearrange("(p c) t -> p c t", p=P)[:, first - QUAD : last - QUAD, :]

        def columns_of(view, first, count):
            if first < QUAD:
                return view[:, :, 0:FRONT].rearrange("p a (m c) -> p a m c", m=P)[:, :, :, first : first + count]
            back = view[:, :, FRONT:N].rearrange("p a (m c) -> p a m c", m=P)
            return back[:, :, :, first - QUAD : first - QUAD + count]

        x4_scale_rows = x4_scales.bitcast(I32).rearrange("a (q s) t -> s q a t", s=4)
        w4_scale_rows = w4_scales.bitcast(I32).rearrange("a (q s) n -> s q a n", s=4)

        nc.sync.dma_start(out=x4_w[:].bitcast(I32), in_=x4_words.bitcast(I32).rearrange("a p b -> p a b"))
        nc.vector.memset(x4_s[:].bitcast(I32), 0)
        nc.vector.memset(w4_s[:].bitcast(I32), 0)
        for s in range(4):
            queue = nc.sync if s == 0 else nc.scalar
            queue.dma_start(out=x4_s[s:P:32, :, :].bitcast(I32), in_=x4_scale_rows[s])
        nc.sync.dma_start(out=w4_w[:].bitcast(I32), in_=w4_words.bitcast(I32).rearrange("a p b -> p a b"))
        for s in range(4):
            queue = nc.sync if s == 0 else nc.scalar
            queue.dma_start(out=w4_s[s:P:32, :, :].bitcast(I32), in_=w4_scale_rows[s])
        nc.sync.dma_start(out=x_raw[0][:], in_=x8_v[0])
        nc.sync.dma_start(out=w_raw[0][:], in_=w8_v[0])
        nc.sync.dma_start(out=x_raw[1][:], in_=x8_v[1])
        w_run = w_raw[1][:].rearrange("p j n -> p (j n)")
        w8_run = w8_v[1].rearrange("p j n -> p (j n)")
        nc.sync.dma_start(out=w_run[:, 0:CUT], in_=w8_run[:, 0:CUT])
        for u, (first, last) in enumerate(R_LOADS):
            nc.sync.dma_start(out=r_sb[u][:], in_=rows_of(r, first, last))
            if u == 0:
                nc.sync.dma_start(out=w_run[:, CUT:], in_=w8_run[:, CUT:])

        def copy(engine, dst, src):
            if engine == "vector":
                nc.vector.tensor_copy(out=dst, in_=src)
            else:
                nc.scalar.copy(out=dst, in_=src)

        def cast_x(g, engine):
            copy(engine, x_grp[g][:], x_raw[g][:].rearrange("p j t -> p t j"))

        def quant_x(g):
            nc.vector.quantize_mx(
                out=x_q[g][:].bitcast(FP8X4), scales=x_s[g][:], in_=x_grp[g][:].rearrange("p t j -> p (t j)")
            )

        def permute(h):
            nc.vector.tensor_copy(
                out=w4_wp[h][:].bitcast(U16).rearrange("p a (i m) -> p a m i", i=QUAD),
                in_=columns_of(w4_w[:].bitcast(U16), h * QUAD, QUAD),
            )
            nc.vector.tensor_copy(
                out=w4_sp[h][:].rearrange("p a (i m) -> p a m i", i=QUAD),
                in_=columns_of(w4_s[:], h * QUAD, QUAD),
            )

        def cast(g, i, engine, count=PAIR):
            src = columns_of(w_raw[g][:], i, count).rearrange("p j m c -> p m j c")
            dst = w_grp[g][:].rearrange("p (c m) j -> p m j c", c=TILES)
            copy(engine, dst[:, :, :, i : i + count], src)

        def quant(g, i, count=PAIR):
            nc.vector.quantize_mx(
                out=w_q[g][:, cols(i, count)].bitcast(FP8X4),
                scales=w_s[g][:, cols(i, count)],
                in_=w_grp[g][:, cols(i, count), :].rearrange("p n j -> p (n j)"),
            )

        acc = {}

        def take_bank(i, bank):
            acc[i] = psum.tile([P, T], F32, name=f"bank{bank}")

        def passes4(i, bank):
            h, c = divmod(i, QUAD)
            take_bank(i, bank)
            for a in range(PASSES4):
                nc.tensor.matmul_mx(
                    out=acc[i][:],
                    lhsT=w4_wp[h][:, a, 2 * c * P : 2 * (c + 1) * P].bitcast(FP4X4),
                    lhsT_scale=w4_sp[h][:, a, cols(c)],
                    rhs=x4_w[:, a, :].bitcast(FP4X4),
                    rhs_scale=x4_s[:, a, :],
                    start=(a == 0),
                    stop=False,
                )

        def pass8(g, i, start=False, stop=False):
            nc.tensor.matmul_mx(
                out=acc[i][:],
                lhsT=w_q[g][:, cols(i)].bitcast(FP8X4),
                lhsT_scale=w_s[g][:, cols(i)],
                rhs=x_q[g][:].bitcast(FP8X4),
                rhs_scale=x_s[g][:],
                start=start,
                stop=stop,
            )

        def finish(i):
            other = parked[:] if i == PARKED else r_of(i)
            nc.vector.tensor_tensor(out=o_sb[:, i, :], in0=acc[i][:], in1=other, op=ADD)
            for first, last in STORES:
                if i == last - 1:
                    nc.sync.dma_start(out=rows_of(out, first, last), in_=o_sb[:, first:last, :])

        def close(*tiles):
            for i in tiles:
                pass8(1, i, stop=True)

        def open_late(i, bank):
            passes4(i, bank)
            pass8(0, i)

        permute(1)
        permute(0)
        for i in (6, 7, 4, 5, 0):
            passes4(i, i)
        cast_x(0, "scalar")
        permute(2)
        quant_x(0)

        cast(0, 6, "vector")
        cast(0, 0, "scalar")
        cast(0, 4, "vector")
        quant(0, 6)
        pass8(0, PARKED, stop=True)
        nc.scalar.copy(out=parked[:], in_=acc[PARKED][:])
        cast(0, 2, "scalar")
        cast(0, 10, "scalar")
        cast(0, 8, "vector")
        for i in (4, 0, 8):
            quant(0, i)
        cast_x(1, "vector")
        quant(0, 2)
        quant_x(1)
        quant(0, 10)
        pass8(0, 7)
        for i in (1, 2, 3):
            passes4(i, i)
        for i in (4, 5, 0, 1, 2, 3):
            pass8(0, i)
        open_late(8, PARKED)

        cast(1, 0, "vector")
        for i in range(2, TILES, PAIR):
            cast(1, i, "scalar")
        quant(1, 0)
        quant(1, 2)
        close(0, 1, 2, 3)
        finish(0)
        finish(1)
        open_late(9, 0)
        finish(2)
        quant(1, 4)
        close(4, 5)
        open_late(10, 1)
        finish(3)
        quant(1, 6)
        take_bank(PARKED, 2)
        pass8(1, PARKED, start=True, stop=True)
        close(7)
        finish(4)
        nc.vector.tensor_tensor(out=parked[:], in0=parked[:], in1=r_of(PARKED), op=ADD)
        finish(5)
        open_late(11, 3)
        finish(6)
        quant(1, 8)
        close(8, 9)
        quant(1, 10)
        close(10, 11)
        for i in range(7, TILES):
            finish(i)
